import numpy as np
import ml_dtypes


def mxq(x, axis, fmt="e4m3"):
    dtype, down = {"e4m3": (ml_dtypes.float8_e4m3fn, 7), "e5m2": (ml_dtypes.float8_e5m2, 14)}[fmt]
    v = np.moveaxis(np.asarray(x, np.float32).astype(ml_dtypes.bfloat16).astype(np.float64), axis, -1)
    blocks = v.reshape(v.shape[:-1] + (-1, 32))
    amax = np.abs(blocks).max(-1, keepdims=True)
    byte = np.maximum(np.where(amax > 0, np.frexp(amax)[1] - 1 + 127, 0) - down, 1)
    scale = np.exp2(byte - 127.0)
    codes = (blocks / scale).astype(np.float32).astype(dtype).astype(np.float64)
    return np.moveaxis((codes * scale).reshape(v.shape), -1, axis)


WIDE = False


def mx_kscale(k):
    if not WIDE:
        return np.ones(k)
    levels = np.array([10, -10, 5, -5, 0])
    if k % 512:
        return np.exp2(np.random.permutation(np.resize(levels, k // 32))).repeat(32)
    a = np.empty((k // 512, 16))
    for p in range(k // 512):
        a[p, :8] = np.random.permutation(np.resize(levels, 8))
        for g in range(8):
            far = levels[np.abs(levels - a[p, g]) >= 10]
            a[p, g + 8] = far[np.random.randint(len(far))]
    return np.exp2(a.ravel()).repeat(32)


def f64(x):
    return np.asarray(x).astype(np.float64)


def striped(idx):
    return np.tile(idx.reshape(-1, 16).T, (8, 1)).astype(np.uint16)


def unstriped(offs):
    return offs[:16].T.reshape(-1).astype(np.int64)


E2M1 = np.array([0.0, 0.5, 1.0, 1.5, 2.0, 3.0, 4.0, 6.0, -0.0, -0.5, -1.0, -1.5, -2.0, -3.0, -4.0, -6.0])


def pack_weight(w, fmt):
    k, n = w.shape
    w = f64(np.asarray(w, np.float32).astype(ml_dtypes.bfloat16)).reshape(k // 32, 32, n)
    amax = np.abs(w).max(1)
    if fmt == "e4m3":
        byte = np.frexp(amax)[1] - 1 + 127 - 7
    else:
        mant, ex = np.frexp(amax / 6.0)
        byte = np.where(mant > 0.5, ex, ex - 1) + 127
    byte = np.clip(np.where(amax > 0, byte, 1), 1, 254)
    scaled = (w * np.exp2(127.0 - byte)[:, None, :]).reshape(k, n).astype(np.float32)
    by_word = np.ascontiguousarray(scaled.reshape(k // 512, 128, 4, n).transpose(0, 1, 3, 2))
    if fmt == "e4m3":
        words = by_word.astype(ml_dtypes.float8_e4m3fn).view(np.uint8)
    else:
        c = by_word.astype(ml_dtypes.float4_e2m1fn).view(np.uint8) & 0xF
        words = (c[..., 0::2] | (c[..., 1::2] << 4)).reshape(k // 512, 128, 2 * n)
    return np.ascontiguousarray(words), np.ascontiguousarray(byte.astype(np.uint8).reshape(k // 512, 16, n))


def unpack_weight(words, scales, fmt):
    g, _, n = scales.shape
    words = np.ascontiguousarray(words).reshape(g, 128, n, -1)
    if fmt == "e4m3":
        vals = words.view(ml_dtypes.float8_e4m3fn).astype(np.float64)
    else:
        nib = np.empty((g, 128, n, 4), np.uint8)
        nib[..., 0::2] = words & 0xF
        nib[..., 1::2] = words >> 4
        vals = E2M1[nib]
    vals = vals * np.repeat(np.exp2(scales.astype(np.float64) - 127.0), 8, axis=1)[..., None]
    return vals.transpose(0, 1, 3, 2).reshape(g * 512, n)


def gelu(v):
    return 0.5 * v * (1.0 + np.tanh(np.sqrt(2.0 / np.pi) * (v + 0.044715 * v**3)))


K, H, N, T, S, P, P2 = 512, 512, 384, 4096, 2048, 1024, 512

def setup_inputs():
    n = np.random.standard_normal
    s = mx_kscale(K)[:, None]
    u = mx_kscale(H)[:, None]
    tab_words, tab_scales = pack_weight(n((K, T)) * s, "e4m3")
    w1 = (n((K, H)) / np.sqrt(K) / s * u.T).astype(np.float32)
    w2_words, w2_scales = pack_weight(n((K, H)) / np.sqrt(K) / s * u.T, "e2m1")
    w3 = (1.5 * n((K, H)) / np.sqrt(K) / s).astype(np.float32)
    w4_words, w4_scales = pack_weight(n((H, N)) / np.sqrt(H) / u, "e4m3")
    return {"tab_words": tab_words, "tab_scales": tab_scales,
            "offs": striped(np.random.permutation(T)[:S]),
            "pos1": striped(np.random.permutation(S)[:P]),
            "pos2": striped(np.random.permutation(S)[:P]),
            "pos3": striped(np.random.permutation(P)[:P2]),
            "pos4": striped(np.random.permutation(S)[:P2]),
            "w1": w1, "w2_words": w2_words, "w2_scales": w2_scales, "w3": w3,
            "w4_words": w4_words, "w4_scales": w4_scales,
            "base": (0.6 * n(N)).astype(np.float32)}

def reference(tab_words, tab_scales, offs, pos1, pos2, pos3, pos4,
              w1, w2_words, w2_scales, w3, w4_words, w4_scales, base):
    v = unpack_weight(tab_words, tab_scales, "e4m3")[:, unstriped(offs)]
    f1 = mxq(f64(w1), 0, "e4m3")
    f2 = unpack_weight(w2_words, w2_scales, "e2m1")
    f3 = mxq(f64(w3), 0, "e4m3")
    f4 = unpack_weight(w4_words, w4_scales, "e4m3")
    h = np.maximum(f1.T @ v, f2.T @ v) * np.tanh(f3.T @ v)
    a1 = h[:, unstriped(pos1)] - h[:, unstriped(pos2)]
    a2 = np.abs(a1[:, unstriped(pos3)]) + h[:, unstriped(pos4)]
    q2 = mxq(a2, 0, "e4m3")
    return (f4.T @ q2) + f64(base)[:, None]

@@ -1,0 +1,172 @@
+from contextlib import ExitStack
+
+import concourse.mybir as mybir
+
+K, H, N, T, S, PAIRS, KEPT = 512, 512, 384, 4096, 2048, 1024, 512
+FLOPS = 2 * 3 * K * H * S + 2 * H * N * KEPT
+
+F32 = mybir.dt.float32
+BF16 = mybir.dt.bfloat16
+I32 = mybir.dt.int32
+U32 = mybir.dt.uint32
+U16 = mybir.dt.uint16
+U8 = mybir.dt.uint8
+FP8X4 = mybir.dt.float8_e4m3fn_x4
+FP4X4 = mybir.dt.float4_e2m1fn_x4
+ALU = mybir.AluOpType
+ACT = mybir.ActivationFunctionType
+
+P = 128
+PACK = 4
+BANK = 512
+PER_COL = 16
+HALF = KEPT // 2
+
+
+def load_scale_rows(queue, plane, rows):
+    for q in range(4):
+        queue.dma_start(out=plane[32 * q : 32 * q + 4, :].bitcast(I32), in_=rows[4 * q : 4 * q + 4, :].bitcast(I32))
+
+
+def tile_list_cartel_bid_screening_kernel(
+    tc, tab_words, tab_scales, offs, pos1, pos2, pos3, pos4, w1, w2_words, w2_scales, w3, w4_words, w4_scales, base, out
+):
+    nc = tc.nc
+    chunks = S // BANK
+    with ExitStack() as ctx:
+        keep = ctx.enter_context(tc.tile_pool(name="keep", bufs=1))
+        ring = ctx.enter_context(tc.tile_pool(name="ring", bufs=2))
+        psum = ctx.enter_context(tc.psum_pool(name="psum", bufs=2))
+
+        idx = keep.tile([P, S // PER_COL], U16, name="idx")
+        p1 = keep.tile([P, PAIRS // PER_COL], U16, name="p1")
+        p2 = keep.tile([P, PAIRS // PER_COL], U16, name="p2")
+        p3 = keep.tile([P, KEPT // PER_COL], U16, name="p3")
+        p4 = keep.tile([P, KEPT // PER_COL], U16, name="p4")
+        tab_w = keep.tile([P, T], U32, name="tab_w", align_bytes=64)
+        tab_s = keep.tile([P, T], U8, name="tab_s", align_bytes=64)
+        w2_raw = keep.tile([P, H], U16, name="w2_raw", align_bytes=64)
+        w2s_raw = keep.tile([P, H], U8, name="w2s_raw", align_bytes=64)
+        w2_w = keep.tile([P, H], U16, name="w2_w", align_bytes=64)
+        w2_s = keep.tile([P, H], U8, name="w2_s", align_bytes=64)
+        w4_w = keep.tile([P, N], U32, name="w4_w", align_bytes=64)
+        w4_s = keep.tile([P, N], U8, name="w4_s", align_bytes=64)
+        bias = keep.tile([P, N // P], F32, name="bias")
+
+        nc.vector.memset(tab_s[:].bitcast(I32), 0)
+        nc.vector.memset(w2s_raw[:].bitcast(I32), 0)
+        nc.vector.memset(w4_s[:].bitcast(I32), 0)
+
+        for tile, src in ((idx, offs), (p2, pos2), (p1, pos1), (p3, pos3), (p4, pos4)):
+            nc.sync.dma_start(tile[:], src)
+        load_scale_rows(nc.sync, tab_s, tab_scales[0])
+        nc.sync.dma_start(out=tab_w[:].bitcast(I32), in_=tab_words[0].rearrange("p t i -> p (t i)").bitcast(I32))
+        nc.sync.dma_start(out=w2_raw[:].bitcast(I32), in_=w2_words[0].bitcast(I32))
+        load_scale_rows(nc.sync, w2s_raw, w2_scales[0])
+        raw = {}
+        for name, w in (("w1", w1), ("w3", w3)):
+            raw[name] = keep.tile([P, PACK, H], F32, name=name + "_raw")
+            nc.sync.dma_start(out=raw[name][:], in_=w.rearrange("(p j) r -> p j r", j=PACK))
+        nc.sync.dma_start(out=w4_w[:].bitcast(I32), in_=w4_words[0].rearrange("p n i -> p (n i)").bitcast(I32))
+        load_scale_rows(nc.sync, w4_s, w4_scales[0])
+        with nc.allow_non_contiguous_dma(reason="one bias value a partition"):
+            nc.sync.dma_start(out=bias[:], in_=base.rearrange("(j p) -> p j", p=P))
+
+        v_w = [keep.tile([P, BANK], U32, name=f"v_w{c}", align_bytes=64) for c in range(chunks)]
+        v_s = [keep.tile([P, BANK], U8, name=f"v_s{c}", align_bytes=64) for c in range(chunks)]
+        cols = BANK // PER_COL
+        for c in range(chunks):
+            nc.vector.tensor_copy(v_s[c][:], tab_s[:].indirect(idx[:, c * cols : (c + 1) * cols]))
+        for c in range(chunks):
+            nc.vector.tensor_copy(v_w[c][:], tab_w[:].indirect(idx[:, c * cols : (c + 1) * cols]))
+
+        nc.vector.tensor_copy(w2_w[:].rearrange("p (t q) -> p t q", t=PACK), w2_raw[:].rearrange("p (q t) -> p t q", t=PACK))
+        nc.vector.tensor_copy(w2_s[:].rearrange("p (t q) -> p t q", t=PACK), w2s_raw[:].rearrange("p (q t) -> p t q", t=PACK))
+
+        codes, scales = {}, {}
+        for t0, t1 in ((0, 1), (1, PACK)):
+            for name in ("w1", "w3"):
+                nt = t1 - t0
+                grouped = keep.tile([P, nt * P * PACK], BF16, name=f"{name}_g{t0}", align_bytes=64)
+                cw = keep.tile([P, nt * P], U32, name=f"{name}_w{t0}", align_bytes=64)
+                cs = keep.tile([P, nt * P], U8, name=f"{name}_s{t0}", align_bytes=64)
+                nc.scalar.copy(
+                    out=grouped[:].rearrange("p (t q j) -> p q t j", t=nt, j=PACK),
+                    in_=raw[name][:].rearrange("p j (q t) -> p q t j", t=PACK)[:, :, t0:t1, :],
+                )
+                nc.vector.quantize_mx(out=cw[:].bitcast(FP8X4), scales=cs[:], in_=grouped[:])
+                for t in range(t0, t1):
+                    codes[name, t] = cw[:, (t - t0) * P : (t - t0 + 1) * P].bitcast(FP8X4)
+                    scales[name, t] = cs[:, (t - t0) * P : (t - t0 + 1) * P]
+        for t in range(PACK):
+            codes["w2", t] = w2_w[:].bitcast(U8)[:, 2 * t * P : 2 * (t + 1) * P].bitcast(FP4X4)
+            scales["w2", t] = w2_s[:, t * P : (t + 1) * P]
+
+        def product(name, t, c, bufs):
+            bank = psum.tile([P, BANK], F32, name="bank_" + name, tag=name, bufs=bufs)
+            nc.tensor.matmul_mx(
+                out=bank[:], lhsT=codes[name, t], lhsT_scale=scales[name, t],
+                rhs=v_w[c][:].bitcast(FP8X4), rhs_scale=v_s[c][:], start=True, stop=True,
+            )
+            return bank
+
+        a2 = [keep.tile([P, PACK, HALF], F32, name=f"a2_{u}") for u in range(2)]
+
+        def features(t):
+            h = ring.tile([P, S], F32, name="h")
+            for c in range(chunks):
+                second = ring.tile([P, BANK], F32, name="second", bufs=4)
+                gate = ring.tile([P, BANK], F32, name="gate", bufs=4)
+                larger = ring.tile([P, BANK], F32, name="larger", bufs=4)
+                bank2 = product("w2", t, c, 2)
+                bank1 = product("w1", t, c, 4)
+                bank3 = product("w3", t, c, 2)
+                nc.scalar.copy(out=second[:], in_=bank2[:])
+                nc.scalar.activation(out=gate[:], in_=bank3[:], func=ACT.Tanh)
+                nc.vector.tensor_tensor(larger[:], bank1[:], second[:], ALU.max)
+                nc.vector.tensor_tensor(h[:, c * BANK : (c + 1) * BANK], larger[:], gate[:], ALU.mult)
+            return h
+
+        def pairs(t, h):
+            other = ring.tile([P, PAIRS], F32, name="other")
+            a1 = ring.tile([P, PAIRS], F32, name="a1")
+            nc.vector.tensor_copy(other[:], h[:].indirect(p2[:]))
+            nc.vector.tensor_tensor(a1[:], h[:].indirect(p1[:]), other[:], ALU.subtract)
+            hc = HALF // PER_COL
+            size = []
+            for u in range(2):
+                kept = ring.tile([P, HALF], F32, name="kept")
+                size.append(ring.tile([P, HALF], F32, name="size"))
+                nc.vector.tensor_copy(kept[:], a1[:].indirect(p3[:, u * hc : (u + 1) * hc]))
+                nc.scalar.activation(out=size[u][:], in_=kept[:], func=ACT.Abs)
+            for u in range(2):
+                nc.vector.tensor_tensor(a2[u][:, t, :], h[:].indirect(p4[:, u * hc : (u + 1) * hc]), size[u][:], ALU.add)
+
+        h = features(0)
+        for t in range(PACK):
+            pairs(t, h)
+            if t + 1 < PACK:
+                h = features(t + 1)
+
+        out_rows = out.rearrange("(j p) m -> p j m", p=P)
+        for u in range(2):
+            woven = keep.tile([P, HALF, PACK], BF16, name=f"woven{u}", align_bytes=64)
+            a2_w = keep.tile([P, HALF], U32, name=f"a2_w{u}", align_bytes=64)
+            a2_s = keep.tile([P, HALF], U8, name=f"a2_s{u}", align_bytes=64)
+            if u == 0:
+                nc.scalar.copy(out=woven[:], in_=a2[u][:].rearrange("p t m -> p m t"))
+            else:
+                nc.vector.tensor_copy(out=woven[:], in_=a2[u][:].rearrange("p t m -> p m t"))
+            nc.vector.quantize_mx(out=a2_w[:].bitcast(FP8X4), scales=a2_s[:], in_=woven[:].rearrange("p m t -> p (m t)"))
+            score = keep.tile([P, N // P, HALF], F32, name=f"score{u}")
+            for j, (name, bufs) in enumerate((("w1", 4), ("w2", 2), ("w3", 2))):
+                bank = psum.tile([P, BANK], F32, name="bank_out", tag=name, bufs=bufs)
+                nc.tensor.matmul_mx(
+                    out=bank[:, :HALF], lhsT=w4_w[:, j * P : (j + 1) * P].bitcast(FP8X4), lhsT_scale=w4_s[:, j * P : (j + 1) * P],
+                    rhs=a2_w[:].bitcast(FP8X4), rhs_scale=a2_s[:], start=True, stop=True,
+                )
+                if u == 1 and j == 1:
+                    nc.vector.tensor_scalar(score[:, j, :], bank[:, :HALF], bias[:, j : j + 1], None, ALU.add)
+                else:
+                    nc.scalar.activation(out=score[:, j, :], in_=bank[:, :HALF], func=ACT.Identity, bias=bias[:, j : j + 1])
+            nc.sync.dma_start(out=out_rows[:, :, u * HALF : (u + 1) * HALF], in_=score[:])

@@ -36,6 +36,7 @@ def tile_list_cartel_bid_screening_kernel(
     with ExitStack() as ctx:
         keep = ctx.enter_context(tc.tile_pool(name="keep", bufs=1))
         ring = ctx.enter_context(tc.tile_pool(name="ring", bufs=2))
+        shared = ctx.enter_context(tc.tile_pool(name="shared", bufs=1))
         psum = ctx.enter_context(tc.psum_pool(name="psum", bufs=2))
 
         idx = keep.tile([P, S // PER_COL], U16, name="idx")
@@ -45,28 +46,27 @@ def tile_list_cartel_bid_screening_kernel(
         p4 = keep.tile([P, KEPT // PER_COL], U16, name="p4")
         tab_w = keep.tile([P, T], U32, name="tab_w", align_bytes=64)
         tab_s = keep.tile([P, T], U8, name="tab_s", align_bytes=64)
-        w2_raw = keep.tile([P, H], U16, name="w2_raw", align_bytes=64)
+        w2_raw = keep.tile([P, 2 * H], U8, name="w2_raw", align_bytes=64)
         w2s_raw = keep.tile([P, H], U8, name="w2s_raw", align_bytes=64)
-        w2_w = keep.tile([P, H], U16, name="w2_w", align_bytes=64)
+        w2_w = keep.tile([P, 2 * H], U8, name="w2_w", align_bytes=64)
         w2_s = keep.tile([P, H], U8, name="w2_s", align_bytes=64)
         w4_w = keep.tile([P, N], U32, name="w4_w", align_bytes=64)
         w4_s = keep.tile([P, N], U8, name="w4_s", align_bytes=64)
         bias = keep.tile([P, N // P], F32, name="bias")
 
         nc.vector.memset(tab_s[:].bitcast(I32), 0)
-        nc.vector.memset(w2s_raw[:].bitcast(I32), 0)
-        nc.vector.memset(w4_s[:].bitcast(I32), 0)
+        nc.gpsimd.memset(w2s_raw[:].bitcast(I32), 0)
+        nc.gpsimd.memset(w4_s[:].bitcast(I32), 0)
 
         for tile, src in ((idx, offs), (p2, pos2), (p1, pos1), (p3, pos3), (p4, pos4)):
             nc.sync.dma_start(tile[:], src)
         load_scale_rows(nc.sync, tab_s, tab_scales[0])
+        raw = {name: keep.tile([P, PACK, H], F32, name=name + "_raw") for name in ("w1", "w3")}
+        nc.sync.dma_start(out=raw["w3"][:], in_=w3.rearrange("(p j) r -> p j r", j=PACK))
         nc.sync.dma_start(out=tab_w[:].bitcast(I32), in_=tab_words[0].rearrange("p t i -> p (t i)").bitcast(I32))
-        nc.sync.dma_start(out=w2_raw[:].bitcast(I32), in_=w2_words[0].bitcast(I32))
         load_scale_rows(nc.sync, w2s_raw, w2_scales[0])
-        raw = {}
-        for name, w in (("w1", w1), ("w3", w3)):
-            raw[name] = keep.tile([P, PACK, H], F32, name=name + "_raw")
-            nc.sync.dma_start(out=raw[name][:], in_=w.rearrange("(p j) r -> p j r", j=PACK))
+        nc.sync.dma_start(out=w2_raw[:].bitcast(I32), in_=w2_words[0].bitcast(I32))
+        nc.sync.dma_start(out=raw["w1"][:], in_=w1.rearrange("(p j) r -> p j r", j=PACK))
         nc.sync.dma_start(out=w4_w[:].bitcast(I32), in_=w4_words[0].rearrange("p n i -> p (n i)").bitcast(I32))
         load_scale_rows(nc.sync, w4_s, w4_scales[0])
         with nc.allow_non_contiguous_dma(reason="one bias value a partition"):
@@ -80,12 +80,17 @@ def tile_list_cartel_bid_screening_kernel(
         for c in range(chunks):
             nc.vector.tensor_copy(v_w[c][:], tab_w[:].indirect(idx[:, c * cols : (c + 1) * cols]))
 
-        nc.vector.tensor_copy(w2_w[:].rearrange("p (t q) -> p t q", t=PACK), w2_raw[:].rearrange("p (q t) -> p t q", t=PACK))
-        nc.vector.tensor_copy(w2_s[:].rearrange("p (t q) -> p t q", t=PACK), w2s_raw[:].rearrange("p (q t) -> p t q", t=PACK))
+        for t in range(PACK):
+            nc.gpsimd.tensor_copy(
+                w2_w[:, 2 * t * P : 2 * (t + 1) * P].rearrange("p (q b) -> p q b", b=2),
+                w2_raw[:].rearrange("p (q t b) -> p t q b", t=PACK, b=2)[:, t, :, :],
+            )
+            nc.gpsimd.tensor_copy(w2_s[:, t * P : (t + 1) * P], w2s_raw[:].rearrange("p (q t) -> p t q", t=PACK)[:, t, :])
 
         codes, scales = {}, {}
-        for t0, t1 in ((0, 1), (1, PACK)):
-            for name in ("w1", "w3"):
+
+        def quantize_weights(names, t0, t1):
+            for name in names:
                 nt = t1 - t0
                 grouped = keep.tile([P, nt * P * PACK], BF16, name=f"{name}_g{t0}", align_bytes=64)
                 cw = keep.tile([P, nt * P], U32, name=f"{name}_w{t0}", align_bytes=64)
@@ -98,8 +103,9 @@ def tile_list_cartel_bid_screening_kernel(
                 for t in range(t0, t1):
                     codes[name, t] = cw[:, (t - t0) * P : (t - t0 + 1) * P].bitcast(FP8X4)
                     scales[name, t] = cs[:, (t - t0) * P : (t - t0 + 1) * P]
+
         for t in range(PACK):
-            codes["w2", t] = w2_w[:].bitcast(U8)[:, 2 * t * P : 2 * (t + 1) * P].bitcast(FP4X4)
+            codes["w2", t] = w2_w[:, 2 * t * P : 2 * (t + 1) * P].bitcast(FP4X4)
             scales["w2", t] = w2_s[:, t * P : (t + 1) * P]
 
         def product(name, t, c, bufs):
@@ -113,40 +119,67 @@ def tile_list_cartel_bid_screening_kernel(
         a2 = [keep.tile([P, PACK, HALF], F32, name=f"a2_{u}") for u in range(2)]
 
         def features(t):
-            h = ring.tile([P, S], F32, name="h")
+            h = ring.tile([P, S], F32, name="h", bufs=3)
+            larger = ring.tile([P, S], F32, name="larger", bufs=2)
             for c in range(chunks):
                 second = ring.tile([P, BANK], F32, name="second", bufs=4)
                 gate = ring.tile([P, BANK], F32, name="gate", bufs=4)
-                larger = ring.tile([P, BANK], F32, name="larger", bufs=4)
                 bank2 = product("w2", t, c, 2)
                 bank1 = product("w1", t, c, 4)
                 bank3 = product("w3", t, c, 2)
                 nc.scalar.copy(out=second[:], in_=bank2[:])
                 nc.scalar.activation(out=gate[:], in_=bank3[:], func=ACT.Tanh)
-                nc.vector.tensor_tensor(larger[:], bank1[:], second[:], ALU.max)
-                nc.vector.tensor_tensor(h[:, c * BANK : (c + 1) * BANK], larger[:], gate[:], ALU.mult)
+                nc.vector.tensor_tensor(larger[:, c * BANK : (c + 1) * BANK], bank1[:], second[:], ALU.max)
+                (nc.vector if (t, c) in () else nc.gpsimd).tensor_tensor(h[:, c * BANK : (c + 1) * BANK], larger[:, c * BANK : (c + 1) * BANK], gate[:], ALU.mult)
             return h
 
         def pairs(t, h):
-            other = ring.tile([P, PAIRS], F32, name="other")
+            last = t == PACK - 1
             a1 = ring.tile([P, PAIRS], F32, name="a1")
-            nc.vector.tensor_copy(other[:], h[:].indirect(p2[:]))
-            nc.vector.tensor_tensor(a1[:], h[:].indirect(p1[:]), other[:], ALU.subtract)
+            pc = BANK // PER_COL
+            for u in range(2):
+                other = ring.tile([P, BANK], F32, name="other")
+                nc.vector.tensor_copy(other[:], h[:].indirect(p2[:, u * pc : (u + 1) * pc]))
+                picked = h[:].indirect(p1[:, u * pc : (u + 1) * pc])
+                if (t, u) in ((3,0),(3,1)):
+                    nc.vector.tensor_tensor(a1[:, u * BANK : (u + 1) * BANK], picked, other[:], ALU.subtract)
+                else:
+                    first = ring.tile([P, BANK], F32, name="first")
+                    nc.vector.tensor_copy(first[:], picked)
+                    nc.gpsimd.tensor_tensor(a1[:, u * BANK : (u + 1) * BANK], first[:], other[:], ALU.subtract)
             hc = HALF // PER_COL
-            size = []
-            for u in range(2):
-                kept = ring.tile([P, HALF], F32, name="kept")
-                size.append(ring.tile([P, HALF], F32, name="size"))
-                nc.vector.tensor_copy(kept[:], a1[:].indirect(p3[:, u * hc : (u + 1) * hc]))
-                nc.scalar.activation(out=size[u][:], in_=kept[:], func=ACT.Abs)
-            for u in range(2):
-                nc.vector.tensor_tensor(a2[u][:, t, :], h[:].indirect(p4[:, u * hc : (u + 1) * hc]), size[u][:], ALU.add)
+            if t in (3,):
+                size = []
+                for u in range(2):
+                    kept = ring.tile([P, HALF], F32, name="kept")
+                    size.append(ring.tile([P, HALF], F32, name="size"))
+                    nc.vector.tensor_copy(kept[:], a1[:].indirect(p3[:, u * hc : (u + 1) * hc]))
+                    nc.scalar.activation(out=size[u][:], in_=kept[:], func=ACT.Abs)
+                for u in range(2):
+                    nc.vector.tensor_tensor(a2[u][:, t, :], h[:].indirect(p4[:, u * hc : (u + 1) * hc]), size[u][:], ALU.add)
+            else:
+                incumbent = ring.tile([P, KEPT], F32, name="incumbent")
+                kept = ring.tile([P, KEPT], F32, name="kept")
+                size = ring.tile([P, KEPT], F32, name="size")
+                nc.vector.tensor_copy(incumbent[:], h[:].indirect(p4[:]))
+                nc.vector.tensor_copy(kept[:], a1[:].indirect(p3[:]))
+                nc.scalar.activation(out=size[:], in_=kept[:], func=ACT.Abs)
+                later.append((t, incumbent, size))
 
-        h = features(0)
+        quantize_weights(("w3",), 0, PACK)
+        quantize_weights(("w1",), 0, 1)
+        later = []
+        hs = [features(0)]
         for t in range(PACK):
-            pairs(t, h)
             if t + 1 < PACK:
-                h = features(t + 1)
+                quantize_weights(("w1",), t + 1, t + 2)
+                hs.append(features(t + 1))
+            for t0, incumbent, size in later:
+                for u in range(2):
+                    cols_u = slice(u * HALF, (u + 1) * HALF)
+                    nc.gpsimd.tensor_tensor(a2[u][:, t0, :], incumbent[:, cols_u], size[:, cols_u], ALU.add)
+            later.clear()
+            pairs(t, hs[t])
 
         out_rows = out.rearrange("(j p) m -> p j m", p=P)
         for u in range(2):

@@ -20,7 +20,7 @@ P = 128
 PACK = 4
 BANK = 512
 PER_COL = 16
-HALF = KEPT // 2
+PARTS = ((0, 128), (128, 384), (384, 512))
 
 
 def load_scale_rows(queue, plane, rows):
@@ -45,7 +45,7 @@ def tile_list_cartel_bid_screening_kernel(
         p3 = keep.tile([P, KEPT // PER_COL], U16, name="p3")
         p4 = keep.tile([P, KEPT // PER_COL], U16, name="p4")
         tab_w = keep.tile([P, T], U32, name="tab_w", align_bytes=64)
-        tab_s = keep.tile([P, T], U8, name="tab_s", align_bytes=64)
+        tab_s = shared.tile([P, T], U8, name="tab_s", align_bytes=64, offset=0)
         w2_raw = keep.tile([P, 2 * H], U8, name="w2_raw", align_bytes=64)
         w2s_raw = keep.tile([P, H], U8, name="w2s_raw", align_bytes=64)
         w2_w = keep.tile([P, 2 * H], U8, name="w2_w", align_bytes=64)
@@ -58,15 +58,15 @@ def tile_list_cartel_bid_screening_kernel(
         nc.gpsimd.memset(w2s_raw[:].bitcast(I32), 0)
         nc.gpsimd.memset(w4_s[:].bitcast(I32), 0)
 
+        raw = {name: keep.tile([P, PACK, H], F32, name=name + "_raw") for name in ("w1", "w3")}
         for tile, src in ((idx, offs), (p2, pos2), (p1, pos1), (p3, pos3), (p4, pos4)):
             nc.sync.dma_start(tile[:], src)
-        load_scale_rows(nc.sync, tab_s, tab_scales[0])
-        raw = {name: keep.tile([P, PACK, H], F32, name=name + "_raw") for name in ("w1", "w3")}
         nc.sync.dma_start(out=raw["w3"][:], in_=w3.rearrange("(p j) r -> p j r", j=PACK))
-        nc.sync.dma_start(out=tab_w[:].bitcast(I32), in_=tab_words[0].rearrange("p t i -> p (t i)").bitcast(I32))
-        load_scale_rows(nc.sync, w2s_raw, w2_scales[0])
-        nc.sync.dma_start(out=w2_raw[:].bitcast(I32), in_=w2_words[0].bitcast(I32))
+        load_scale_rows(nc.sync, tab_s, tab_scales[0])
         nc.sync.dma_start(out=raw["w1"][:], in_=w1.rearrange("(p j) r -> p j r", j=PACK))
+        nc.sync.dma_start(out=w2_raw[:].bitcast(I32), in_=w2_words[0].bitcast(I32))
+        load_scale_rows(nc.sync, w2s_raw, w2_scales[0])
+        nc.sync.dma_start(out=tab_w[:].bitcast(I32), in_=tab_words[0].rearrange("p t i -> p (t i)").bitcast(I32))
         nc.sync.dma_start(out=w4_w[:].bitcast(I32), in_=w4_words[0].rearrange("p n i -> p (n i)").bitcast(I32))
         load_scale_rows(nc.sync, w4_s, w4_scales[0])
         with nc.allow_non_contiguous_dma(reason="one bias value a partition"):
@@ -93,7 +93,7 @@ def tile_list_cartel_bid_screening_kernel(
             for name in names:
                 nt = t1 - t0
                 grouped = keep.tile([P, nt * P * PACK], BF16, name=f"{name}_g{t0}", align_bytes=64)
-                cw = keep.tile([P, nt * P], U32, name=f"{name}_w{t0}", align_bytes=64)
+                cw = shared.tile([P, nt * P], U32, name=f"{name}_w{t0}", align_bytes=64, offset=2048 * (name == "w1"))
                 cs = keep.tile([P, nt * P], U8, name=f"{name}_s{t0}", align_bytes=64)
                 nc.scalar.copy(
                     out=grouped[:].rearrange("p (t q j) -> p q t j", t=nt, j=PACK),
@@ -116,7 +116,7 @@ def tile_list_cartel_bid_screening_kernel(
             )
             return bank
 
-        a2 = [keep.tile([P, PACK, HALF], F32, name=f"a2_{u}") for u in range(2)]
+        a2 = keep.tile([P, PACK, KEPT], F32, name="a2")
 
         def features(t):
             h = ring.tile([P, S], F32, name="h", bufs=3)
@@ -130,15 +130,45 @@ def tile_list_cartel_bid_screening_kernel(
                 nc.scalar.copy(out=second[:], in_=bank2[:])
                 nc.scalar.activation(out=gate[:], in_=bank3[:], func=ACT.Tanh)
                 nc.vector.tensor_tensor(larger[:, c * BANK : (c + 1) * BANK], bank1[:], second[:], ALU.max)
-                (nc.vector if (t, c) in () else nc.gpsimd).tensor_tensor(h[:, c * BANK : (c + 1) * BANK], larger[:, c * BANK : (c + 1) * BANK], gate[:], ALU.mult)
+                (nc.vector if (t, c) in ((0,2),(0,3)) else nc.gpsimd).tensor_tensor(h[:, c * BANK : (c + 1) * BANK], larger[:, c * BANK : (c + 1) * BANK], gate[:], ALU.mult)
             return h
+
+        out_rows = out.rearrange("(j p) m -> p j m", p=P)
+
+        def scores(u):
+            m0, m1 = PARTS[u]
+            width = m1 - m0
+            woven = keep.tile([P, width, PACK], BF16, name=f"woven{u}", align_bytes=64)
+            a2_w = keep.tile([P, width], U32, name=f"a2_w{u}", align_bytes=64)
+            a2_s = keep.tile([P, width], U8, name=f"a2_s{u}", align_bytes=64)
+            if u in (0,):
+                nc.scalar.copy(out=woven[:], in_=a2[:, :, m0:m1].rearrange("p t m -> p m t"))
+            else:
+                nc.vector.tensor_copy(out=woven[:], in_=a2[:, :, m0:m1].rearrange("p t m -> p m t"))
+            nc.vector.quantize_mx(out=a2_w[:].bitcast(FP8X4), scales=a2_s[:], in_=woven[:].rearrange("p m t -> p (m t)"))
+            score = keep.tile([P, N // P, width], F32, name=f"score{u}")
+            on_scalar = (2, 2, 1)[u]
+            for js, name, bufs in ((range(on_scalar), "w1", 4), (range(on_scalar, N // P), ("w1", "w2", "w3")[u], (4, 2, 2)[u])):
+                bank = psum.tile([P, BANK], F32, name="bank_out", tag=name, bufs=bufs)
+                for i, j in enumerate(js):
+                    nc.tensor.matmul_mx(
+                        out=bank[:, i * width : (i + 1) * width], lhsT=w4_w[:, j * P : (j + 1) * P].bitcast(FP8X4), lhsT_scale=w4_s[:, j * P : (j + 1) * P],
+                        rhs=a2_w[:].bitcast(FP8X4), rhs_scale=a2_s[:], start=True, stop=True,
+                    )
+                for i, j in enumerate(js):
+                    sums = bank[:, i * width : (i + 1) * width]
+                    if j < on_scalar:
+                        nc.scalar.activation(out=score[:, j, :], in_=sums, func=ACT.Identity, bias=bias[:, j : j + 1])
+                    else:
+                        nc.vector.tensor_scalar(score[:, j, :], sums, bias[:, j : j + 1], None, ALU.add)
+            nc.sync.dma_start(out=out_rows[:, :, m0:m1], in_=score[:])
 
         def pairs(t, h):
             last = t == PACK - 1
-            a1 = ring.tile([P, PAIRS], F32, name="a1")
+            a1 = ring.tile([P, PAIRS], F32, name="a1", bufs=1)
             pc = BANK // PER_COL
             for u in range(2):
-                other = ring.tile([P, BANK], F32, name="other")
+                other = ring.tile([P, BANK], F32, name="other_last" if last else "other")
                 nc.vector.tensor_copy(other[:], h[:].indirect(p2[:, u * pc : (u + 1) * pc]))
                 picked = h[:].indirect(p1[:, u * pc : (u + 1) * pc])
                 if (t, u) in ((3,0),(3,1)):
@@ -147,16 +177,18 @@ def tile_list_cartel_bid_screening_kernel(
                     first = ring.tile([P, BANK], F32, name="first")
                     nc.vector.tensor_copy(first[:], picked)
                     nc.gpsimd.tensor_tensor(a1[:, u * BANK : (u + 1) * BANK], first[:], other[:], ALU.subtract)
-            hc = HALF // PER_COL
-            if t in (3,):
-                size = []
-                for u in range(2):
-                    kept = ring.tile([P, HALF], F32, name="kept")
-                    size.append(ring.tile([P, HALF], F32, name="size"))
-                    nc.vector.tensor_copy(kept[:], a1[:].indirect(p3[:, u * hc : (u + 1) * hc]))
-                    nc.scalar.activation(out=size[u][:], in_=kept[:], func=ACT.Abs)
-                for u in range(2):
-                    nc.vector.tensor_tensor(a2[u][:, t, :], h[:].indirect(p4[:, u * hc : (u + 1) * hc]), size[u][:], ALU.add)
+            if last:
+                size = keep.tile([P, KEPT], F32, name="size_last")
+                kept = keep.tile([P, KEPT], F32, name="kept_last")
+                for u in range(len(PARTS) + 1):
+                    if u < len(PARTS):
+                        m0, m1 = PARTS[u]
+                        nc.vector.tensor_copy(kept[:, m0:m1], a1[:].indirect(p3[:, m0 // PER_COL : m1 // PER_COL]))
+                        nc.scalar.activation(out=size[:, m0:m1], in_=kept[:, m0:m1], func=ACT.Abs)
+                    if u > 0:
+                        m0, m1 = PARTS[u - 1]
+                        nc.vector.tensor_tensor(a2[:, t, m0:m1], h[:].indirect(p4[:, m0 // PER_COL : m1 // PER_COL]), size[:, m0:m1], ALU.add)
+                        scores(u - 1)
             else:
                 incumbent = ring.tile([P, KEPT], F32, name="incumbent")
                 kept = ring.tile([P, KEPT], F32, name="kept")
@@ -166,40 +198,13 @@ def tile_list_cartel_bid_screening_kernel(
                 nc.scalar.activation(out=size[:], in_=kept[:], func=ACT.Abs)
                 later.append((t, incumbent, size))
 
-        quantize_weights(("w3",), 0, PACK)
-        quantize_weights(("w1",), 0, 1)
+        quantize_weights(("w3", "w1"), 0, PACK)
         later = []
         hs = [features(0)]
         for t in range(PACK):
             if t + 1 < PACK:
-                quantize_weights(("w1",), t + 1, t + 2)
                 hs.append(features(t + 1))
             for t0, incumbent, size in later:
-                for u in range(2):
-                    cols_u = slice(u * HALF, (u + 1) * HALF)
-                    nc.gpsimd.tensor_tensor(a2[u][:, t0, :], incumbent[:, cols_u], size[:, cols_u], ALU.add)
+                nc.gpsimd.tensor_tensor(a2[:, t0, :], incumbent[:], size[:], ALU.add)
             later.clear()
             pairs(t, hs[t])
-
-        out_rows = out.rearrange("(j p) m -> p j m", p=P)
-        for u in range(2):
-            woven = keep.tile([P, HALF, PACK], BF16, name=f"woven{u}", align_bytes=64)
-            a2_w = keep.tile([P, HALF], U32, name=f"a2_w{u}", align_bytes=64)
-            a2_s = keep.tile([P, HALF], U8, name=f"a2_s{u}", align_bytes=64)
-            if u == 0:
-                nc.scalar.copy(out=woven[:], in_=a2[u][:].rearrange("p t m -> p m t"))
-            else:
-                nc.vector.tensor_copy(out=woven[:], in_=a2[u][:].rearrange("p t m -> p m t"))
-            nc.vector.quantize_mx(out=a2_w[:].bitcast(FP8X4), scales=a2_s[:], in_=woven[:].rearrange("p m t -> p (m t)"))
-            score = keep.tile([P, N // P, HALF], F32, name=f"score{u}")
-            for j, (name, bufs) in enumerate((("w1", 4), ("w2", 2), ("w3", 2))):
-                bank = psum.tile([P, BANK], F32, name="bank_out", tag=name, bufs=bufs)
-                nc.tensor.matmul_mx(
-                    out=bank[:, :HALF], lhsT=w4_w[:, j * P : (j + 1) * P].bitcast(FP8X4), lhsT_scale=w4_s[:, j * P : (j + 1) * P],
-                    rhs=a2_w[:].bitcast(FP8X4), rhs_scale=a2_s[:], start=True, stop=True,
-                )
-                if u == 1 and j == 1:
-                    nc.vector.tensor_scalar(score[:, j, :], bank[:, :HALF], bias[:, j : j + 1], None, ALU.add)
-                else:
-                    nc.scalar.activation(out=score[:, j, :], in_=bank[:, :HALF], func=ACT.Identity, bias=bias[:, j : j + 1])
-            nc.sync.dma_start(out=out_rows[:, :, u * HALF : (u + 1) * HALF], in_=score[:])

@@ -19,20 +19,38 @@ ACT = mybir.ActivationFunctionType
 P = 128
 PACK = 4
 BANK = 512
+CHUNKS = S // BANK
 PER_COL = 16
-PARTS = ((0, 128), (128, 384), (384, 512))
+CHUNK_BYTES = 4 * BANK
+
+BANKS = {"w1": 4, "w2": 2, "w3": 2}
+AHEAD = 2
+PARTS = [(m0, m0 + P) for m0 in range(0, KEPT, P)]
+ON_SCALAR = 2
+
+WORDS_AT = T
+STAGE_AT = WORDS_AT + CHUNKS * CHUNK_BYTES
+SLICE_BYTES = CHUNKS * CHUNK_BYTES
+LARGER_AT = STAGE_AT + PACK * SLICE_BYTES
 
 
-def load_scale_rows(queue, plane, rows):
-    for q in range(4):
-        queue.dma_start(out=plane[32 * q : 32 * q + 4, :].bitcast(I32), in_=rows[4 * q : 4 * q + 4, :].bitcast(I32))
+def load_scale_rows(nc, plane, rows):
+    for r in range(4):
+        nc.sync.dma_start(out=plane[r:P:32, :].bitcast(I32), in_=rows[r:16:4, :].bitcast(I32))
+
+
+def entries(lst, first, end):
+    return lst[:, first // PER_COL : end // PER_COL]
+
+
+def chunk(tile, c):
+    return tile[:, c * BANK : (c + 1) * BANK]
 
 
 def tile_list_cartel_bid_screening_kernel(
     tc, tab_words, tab_scales, offs, pos1, pos2, pos3, pos4, w1, w2_words, w2_scales, w3, w4_words, w4_scales, base, out
 ):
     nc = tc.nc
-    chunks = S // BANK
     with ExitStack() as ctx:
         keep = ctx.enter_context(tc.tile_pool(name="keep", bufs=1))
         ring = ctx.enter_context(tc.tile_pool(name="ring", bufs=2))
@@ -53,158 +71,176 @@ def tile_list_cartel_bid_screening_kernel(
         w4_w = keep.tile([P, N], U32, name="w4_w", align_bytes=64)
         w4_s = keep.tile([P, N], U8, name="w4_s", align_bytes=64)
         bias = keep.tile([P, N // P], F32, name="bias")
+        raw = {name: keep.tile([P, PACK, H], F32, name=name + "_raw") for name in ("w1", "w3")}
 
         nc.vector.memset(tab_s[:].bitcast(I32), 0)
         nc.gpsimd.memset(w2s_raw[:].bitcast(I32), 0)
         nc.gpsimd.memset(w4_s[:].bitcast(I32), 0)
 
-        raw = {name: keep.tile([P, PACK, H], F32, name=name + "_raw") for name in ("w1", "w3")}
-        for tile, src in ((idx, offs), (p2, pos2), (p1, pos1), (p3, pos3), (p4, pos4)):
-            nc.sync.dma_start(tile[:], src)
+        for lst, src in ((idx, offs), (p2, pos2), (p1, pos1), (p3, pos3), (p4, pos4)):
+            nc.sync.dma_start(lst[:], src)
         nc.sync.dma_start(out=raw["w3"][:], in_=w3.rearrange("(p j) r -> p j r", j=PACK))
-        load_scale_rows(nc.sync, tab_s, tab_scales[0])
+        load_scale_rows(nc, tab_s, tab_scales[0])
         nc.sync.dma_start(out=raw["w1"][:], in_=w1.rearrange("(p j) r -> p j r", j=PACK))
         nc.sync.dma_start(out=w2_raw[:].bitcast(I32), in_=w2_words[0].bitcast(I32))
-        load_scale_rows(nc.sync, w2s_raw, w2_scales[0])
+        load_scale_rows(nc, w2s_raw, w2_scales[0])
         nc.sync.dma_start(out=tab_w[:].bitcast(I32), in_=tab_words[0].rearrange("p t i -> p (t i)").bitcast(I32))
         nc.sync.dma_start(out=w4_w[:].bitcast(I32), in_=w4_words[0].rearrange("p n i -> p (n i)").bitcast(I32))
-        load_scale_rows(nc.sync, w4_s, w4_scales[0])
-        with nc.allow_non_contiguous_dma(reason="one bias value a partition"):
+        load_scale_rows(nc, w4_s, w4_scales[0])
+        with nc.allow_non_contiguous_dma(reason="one value of base for each partition and row tile"):
             nc.sync.dma_start(out=bias[:], in_=base.rearrange("(j p) -> p j", p=P))
 
-        v_w = [keep.tile([P, BANK], U32, name=f"v_w{c}", align_bytes=64) for c in range(chunks)]
-        v_s = [keep.tile([P, BANK], U8, name=f"v_s{c}", align_bytes=64) for c in range(chunks)]
-        cols = BANK // PER_COL
-        for c in range(chunks):
-            nc.vector.tensor_copy(v_s[c][:], tab_s[:].indirect(idx[:, c * cols : (c + 1) * cols]))
-        for c in range(chunks):
-            nc.vector.tensor_copy(v_w[c][:], tab_w[:].indirect(idx[:, c * cols : (c + 1) * cols]))
+        v_s = [keep.tile([P, BANK], U8, name=f"v_s{c}", align_bytes=64) for c in range(CHUNKS)]
+        for c in range(CHUNKS):
+            nc.vector.tensor_copy(v_s[c][:], tab_s[:].indirect(entries(idx, c * BANK, (c + 1) * BANK)))
 
-        for t in range(PACK):
-            nc.gpsimd.tensor_copy(
-                w2_w[:, 2 * t * P : 2 * (t + 1) * P].rearrange("p (q b) -> p q b", b=2),
-                w2_raw[:].rearrange("p (q t b) -> p t q b", t=PACK, b=2)[:, t, :, :],
+        v_w = {}
+
+        def gather_words(c):
+            v_w[c] = shared.tile([P, BANK], U32, name=f"v_w{c}", align_bytes=64, offset=WORDS_AT + c * CHUNK_BYTES)
+            nc.vector.tensor_copy(v_w[c][:], tab_w[:].indirect(entries(idx, c * BANK, (c + 1) * BANK)))
+
+        for c in range(AHEAD):
+            gather_words(c)
+
+        nc.vector.tensor_copy(
+            w2_w[:].bitcast(U16).rearrange("p (t q) -> p t q", t=PACK), w2_raw[:].bitcast(U16).rearrange("p (q t) -> p t q", t=PACK)
+        )
+        nc.vector.tensor_copy(w2_s[:].rearrange("p (t q) -> p t q", t=PACK), w2s_raw[:].rearrange("p (q t) -> p t q", t=PACK))
+        stationary = {
+            ("w2", t): (w2_w[:, 2 * t * P : 2 * (t + 1) * P].bitcast(FP4X4), w2_s[:, t * P : (t + 1) * P]) for t in range(PACK)
+        }
+
+        for half, name in enumerate(("w3", "w1")):
+            rounded = keep.tile([P, H * PACK], BF16, name=name + "_rounded", align_bytes=64)
+            codes = shared.tile([P, H], U32, name=name + "_codes", align_bytes=64, offset=half * T // 2)
+            scales = keep.tile([P, H], U8, name=name + "_scales", align_bytes=64)
+            nc.scalar.copy(
+                out=rounded[:].rearrange("p (t q j) -> p q t j", t=PACK, j=PACK),
+                in_=raw[name][:].rearrange("p j (q t) -> p q t j", t=PACK),
             )
-            nc.gpsimd.tensor_copy(w2_s[:, t * P : (t + 1) * P], w2s_raw[:].rearrange("p (q t) -> p t q", t=PACK)[:, t, :])
+            nc.vector.quantize_mx(out=codes[:].bitcast(FP8X4), scales=scales[:], in_=rounded[:])
+            for t in range(PACK):
+                stationary[name, t] = (codes[:, t * P : (t + 1) * P].bitcast(FP8X4), scales[:, t * P : (t + 1) * P])
 
-        codes, scales = {}, {}
-
-        def quantize_weights(names, t0, t1):
-            for name in names:
-                nt = t1 - t0
-                grouped = keep.tile([P, nt * P * PACK], BF16, name=f"{name}_g{t0}", align_bytes=64)
-                cw = shared.tile([P, nt * P], U32, name=f"{name}_w{t0}", align_bytes=64, offset=2048 * (name == "w1"))
-                cs = keep.tile([P, nt * P], U8, name=f"{name}_s{t0}", align_bytes=64)
-                nc.scalar.copy(
-                    out=grouped[:].rearrange("p (t q j) -> p q t j", t=nt, j=PACK),
-                    in_=raw[name][:].rearrange("p j (q t) -> p q t j", t=PACK)[:, :, t0:t1, :],
-                )
-                nc.vector.quantize_mx(out=cw[:].bitcast(FP8X4), scales=cs[:], in_=grouped[:])
-                for t in range(t0, t1):
-                    codes[name, t] = cw[:, (t - t0) * P : (t - t0 + 1) * P].bitcast(FP8X4)
-                    scales[name, t] = cs[:, (t - t0) * P : (t - t0 + 1) * P]
-
-        for t in range(PACK):
-            codes["w2", t] = w2_w[:, 2 * t * P : 2 * (t + 1) * P].bitcast(FP4X4)
-            scales["w2", t] = w2_s[:, t * P : (t + 1) * P]
-
-        def product(name, t, c, bufs):
-            bank = psum.tile([P, BANK], F32, name="bank_" + name, tag=name, bufs=bufs)
+        def product(name, t, c):
+            bank = psum.tile([P, BANK], F32, name="bank_" + name, tag=name, bufs=BANKS[name])
+            lhs_codes, lhs_scales = stationary[name, t]
             nc.tensor.matmul_mx(
-                out=bank[:], lhsT=codes[name, t], lhsT_scale=scales[name, t],
+                out=bank[:], lhsT=lhs_codes, lhsT_scale=lhs_scales,
                 rhs=v_w[c][:].bitcast(FP8X4), rhs_scale=v_s[c][:], start=True, stop=True,
             )
             return bank
 
-        a2 = keep.tile([P, PACK, KEPT], F32, name="a2")
+        seconds = {}
+
+        def copy_second(t, c):
+            if t == 0 and c + AHEAD < CHUNKS:
+                place = WORDS_AT + (c + AHEAD) * CHUNK_BYTES
+            else:
+                place = STAGE_AT + t * SLICE_BYTES + c * CHUNK_BYTES
+            seconds[t, c] = shared.tile([P, BANK], F32, name=f"second{t}_{c}", align_bytes=64, offset=place)
+            nc.scalar.copy(out=seconds[t, c][:], in_=product("w2", t, c)[:])
+
+        def maximum(t, c, larger):
+            if (t, c) not in seconds:
+                copy_second(t, c)
+            nc.vector.tensor_tensor(chunk(larger, c), product("w1", t, c)[:], seconds[t, c][:], ALU.max)
+
+        def gated(t, c, larger):
+            gate = ring.tile([P, BANK], F32, name="gate", bufs=CHUNKS)
+            nc.scalar.activation(out=gate[:], in_=product("w3", t, c)[:], func=ACT.Tanh)
+            nc.gpsimd.tensor_tensor(chunk(h[t], c), chunk(larger, c), gate[:], ALU.mult)
 
         def features(t):
-            h = ring.tile([P, S], F32, name="h", bufs=3)
-            larger = ring.tile([P, S], F32, name="larger", bufs=2)
-            for c in range(chunks):
-                second = ring.tile([P, BANK], F32, name="second", bufs=4)
-                gate = ring.tile([P, BANK], F32, name="gate", bufs=4)
-                bank2 = product("w2", t, c, 2)
-                bank1 = product("w1", t, c, 4)
-                bank3 = product("w3", t, c, 2)
-                nc.scalar.copy(out=second[:], in_=bank2[:])
-                nc.scalar.activation(out=gate[:], in_=bank3[:], func=ACT.Tanh)
-                nc.vector.tensor_tensor(larger[:, c * BANK : (c + 1) * BANK], bank1[:], second[:], ALU.max)
-                (nc.vector if (t, c) in ((0,2),(0,3)) else nc.gpsimd).tensor_tensor(h[:, c * BANK : (c + 1) * BANK], larger[:, c * BANK : (c + 1) * BANK], gate[:], ALU.mult)
-            return h
+            h[t] = keep.tile([P, S], F32, name=f"h{t}")
+            larger = shared.tile([P, S], F32, name=f"larger{t}", align_bytes=64, offset=LARGER_AT + t % 2 * SLICE_BYTES)
+            for c in range(CHUNKS):
+                if t == 0 and c >= AHEAD:
+                    copy_second(1, c - AHEAD)
+                maximum(t, c, larger)
+                if t == 0:
+                    gated(t, c, larger)
+                if t == 0 and c + AHEAD < CHUNKS:
+                    gather_words(c + AHEAD)
+            if t > 0:
+                for c in range(CHUNKS):
+                    gated(t, c, larger)
 
+        a2 = shared.tile([P, PACK, KEPT], F32, name="a2", align_bytes=64, offset=LARGER_AT + SLICE_BYTES + 4 * PAIRS)
         out_rows = out.rearrange("(j p) m -> p j m", p=P)
 
-        def scores(u):
-            m0, m1 = PARTS[u]
+        def scores(part):
+            m0, m1 = PARTS[part]
             width = m1 - m0
-            woven = keep.tile([P, width, PACK], BF16, name=f"woven{u}", align_bytes=64)
-            a2_w = keep.tile([P, width], U32, name=f"a2_w{u}", align_bytes=64)
-            a2_s = keep.tile([P, width], U8, name=f"a2_s{u}", align_bytes=64)
-            if u in (0,):
-                nc.scalar.copy(out=woven[:], in_=a2[:, :, m0:m1].rearrange("p t m -> p m t"))
+            woven = keep.tile([P, width, PACK], BF16, name=f"woven{part}", align_bytes=64)
+            a2_w = keep.tile([P, width], U32, name=f"a2_w{part}", align_bytes=64)
+            a2_s = keep.tile([P, width], U8, name=f"a2_s{part}", align_bytes=64)
+            by_column = a2[:, :, m0:m1].rearrange("p t m -> p m t")
+            if part < len(PARTS) // 2:
+                nc.scalar.copy(out=woven[:], in_=by_column)
             else:
-                nc.vector.tensor_copy(out=woven[:], in_=a2[:, :, m0:m1].rearrange("p t m -> p m t"))
+                nc.vector.tensor_copy(out=woven[:], in_=by_column)
             nc.vector.quantize_mx(out=a2_w[:].bitcast(FP8X4), scales=a2_s[:], in_=woven[:].rearrange("p m t -> p (m t)"))
-            score = keep.tile([P, N // P, width], F32, name=f"score{u}")
-            on_scalar = (2, 2, 1)[u]
-            for js, name, bufs in ((range(on_scalar), "w1", 4), (range(on_scalar, N // P), ("w1", "w2", "w3")[u], (4, 2, 2)[u])):
-                bank = psum.tile([P, BANK], F32, name="bank_out", tag=name, bufs=bufs)
-                for i, j in enumerate(js):
+            score = keep.tile([P, N // P, width], F32, name=f"score{part}")
+            for row_tiles, tag in ((range(ON_SCALAR), "w1"), (range(ON_SCALAR, N // P), ("w2", "w3")[part % 2])):
+                bank = psum.tile([P, BANK], F32, name="bank_out", tag=tag, bufs=BANKS[tag])
+                for i, j in enumerate(row_tiles):
                     nc.tensor.matmul_mx(
-                        out=bank[:, i * width : (i + 1) * width], lhsT=w4_w[:, j * P : (j + 1) * P].bitcast(FP8X4), lhsT_scale=w4_s[:, j * P : (j + 1) * P],
+                        out=bank[:, i * width : (i + 1) * width],
+                        lhsT=w4_w[:, j * P : (j + 1) * P].bitcast(FP8X4), lhsT_scale=w4_s[:, j * P : (j + 1) * P],
                         rhs=a2_w[:].bitcast(FP8X4), rhs_scale=a2_s[:], start=True, stop=True,
                     )
-                for i, j in enumerate(js):
+                for i, j in enumerate(row_tiles):
                     sums = bank[:, i * width : (i + 1) * width]
-                    if j < on_scalar:
+                    if j < ON_SCALAR:
                         nc.scalar.activation(out=score[:, j, :], in_=sums, func=ACT.Identity, bias=bias[:, j : j + 1])
                     else:
                         nc.vector.tensor_scalar(score[:, j, :], sums, bias[:, j : j + 1], None, ALU.add)
             nc.sync.dma_start(out=out_rows[:, :, m0:m1], in_=score[:])
 
-        def pairs(t, h):
+        def pairs(t):
             last = t == PACK - 1
-            a1 = ring.tile([P, PAIRS], F32, name="a1", bufs=1)
-            pc = BANK // PER_COL
-            for u in range(2):
-                other = ring.tile([P, BANK], F32, name="other_last" if last else "other")
-                nc.vector.tensor_copy(other[:], h[:].indirect(p2[:, u * pc : (u + 1) * pc]))
-                picked = h[:].indirect(p1[:, u * pc : (u + 1) * pc])
-                if (t, u) in ((3,0),(3,1)):
-                    nc.vector.tensor_tensor(a1[:, u * BANK : (u + 1) * BANK], picked, other[:], ALU.subtract)
+            a1 = shared.tile([P, PAIRS], F32, name=f"a1_{t}", align_bytes=64, offset=LARGER_AT + min(t + 1, PACK - 1) % 2 * SLICE_BYTES)
+            picks = shared.tile([P, S], F32, name=f"picks{t}", align_bytes=64, offset=STAGE_AT + (t + 1) % PACK * SLICE_BYTES)
+            for c in range(PAIRS // BANK):
+                by_p1 = h[t][:].indirect(entries(p1, c * BANK, (c + 1) * BANK))
+                other = chunk(picks, 2 * c)
+                nc.vector.tensor_copy(other, h[t][:].indirect(entries(p2, c * BANK, (c + 1) * BANK)))
+                if last:
+                    nc.vector.tensor_tensor(chunk(a1, c), by_p1, other, ALU.subtract)
                 else:
-                    first = ring.tile([P, BANK], F32, name="first")
-                    nc.vector.tensor_copy(first[:], picked)
-                    nc.gpsimd.tensor_tensor(a1[:, u * BANK : (u + 1) * BANK], first[:], other[:], ALU.subtract)
+                    first = chunk(picks, 2 * c + 1)
+                    nc.vector.tensor_copy(first, by_p1)
+                    nc.gpsimd.tensor_tensor(chunk(a1, c), first, other, ALU.subtract)
+            kept[t] = keep.tile([P, KEPT], F32, name=f"kept{t}")
             if last:
                 size = keep.tile([P, KEPT], F32, name="size_last")
-                kept = keep.tile([P, KEPT], F32, name="kept_last")
-                for u in range(len(PARTS) + 1):
-                    if u < len(PARTS):
-                        m0, m1 = PARTS[u]
-                        nc.vector.tensor_copy(kept[:, m0:m1], a1[:].indirect(p3[:, m0 // PER_COL : m1 // PER_COL]))
-                        nc.scalar.activation(out=size[:, m0:m1], in_=kept[:, m0:m1], func=ACT.Abs)
-                    if u > 0:
-                        m0, m1 = PARTS[u - 1]
-                        nc.vector.tensor_tensor(a2[:, t, m0:m1], h[:].indirect(p4[:, m0 // PER_COL : m1 // PER_COL]), size[:, m0:m1], ALU.add)
-                        scores(u - 1)
-            else:
-                incumbent = ring.tile([P, KEPT], F32, name="incumbent")
-                kept = ring.tile([P, KEPT], F32, name="kept")
-                size = ring.tile([P, KEPT], F32, name="size")
-                nc.vector.tensor_copy(incumbent[:], h[:].indirect(p4[:]))
-                nc.vector.tensor_copy(kept[:], a1[:].indirect(p3[:]))
-                nc.scalar.activation(out=size[:], in_=kept[:], func=ACT.Abs)
-                later.append((t, incumbent, size))
+                for part in range(len(PARTS) + 1):
+                    if part < len(PARTS):
+                        m0, m1 = PARTS[part]
+                        nc.vector.tensor_copy(kept[t][:, m0:m1], a1[:].indirect(entries(p3, m0, m1)))
+                        nc.scalar.activation(out=size[:, m0:m1], in_=kept[t][:, m0:m1], func=ACT.Abs)
+                    if part > 0:
+                        m0, m1 = PARTS[part - 1]
+                        nc.vector.tensor_tensor(a2[:, t, m0:m1], h[t][:].indirect(entries(p4, m0, m1)), size[:, m0:m1], ALU.add)
+                        scores(part - 1)
+                return
+            if t == 0:
+                nc.vector.tensor_copy(incumbent[:], h[t][:].indirect(p4[:]))
+            nc.vector.tensor_copy(kept[t][:], a1[:].indirect(p3[:]))
+            if t == PACK - 2:
+                nc.scalar.activation(out=a2[:, 0, :], in_=kept[0][:], func=ACT.Abs)
+                nc.gpsimd.tensor_tensor(a2[:, 0, :], a2[:, 0, :], incumbent[:], ALU.add)
+                sizes = shared.tile([P, t, KEPT], F32, name="sizes", align_bytes=64, offset=STAGE_AT + (t + 1) * SLICE_BYTES)
+                for earlier in range(1, t + 1):
+                    nc.scalar.activation(out=sizes[:, earlier - 1, :], in_=kept[earlier][:], func=ACT.Abs)
+                    nc.vector.tensor_tensor(a2[:, earlier, :], h[earlier][:].indirect(p4[:]), sizes[:, earlier - 1, :], ALU.add)
 
-        quantize_weights(("w3", "w1"), 0, PACK)
-        later = []
-        hs = [features(0)]
+        incumbent = keep.tile([P, KEPT], F32, name="incumbent")
+        h, kept = {}, {}
+        features(0)
         for t in range(PACK):
             if t + 1 < PACK:
-                hs.append(features(t + 1))
-            for t0, incumbent, size in later:
-                nc.gpsimd.tensor_tensor(a2[:, t0, :], incumbent[:], size[:], ALU.add)
-            later.clear()
-            pairs(t, hs[t])
+                features(t + 1)
+            pairs(t)

from contextlib import ExitStack

import concourse.mybir as mybir

K, H, N, T, S, PAIRS, KEPT = 512, 512, 384, 4096, 2048, 1024, 512
FLOPS = 2 * 3 * K * H * S + 2 * H * N * KEPT

F32 = mybir.dt.float32
BF16 = mybir.dt.bfloat16
I32 = mybir.dt.int32
U32 = mybir.dt.uint32
U16 = mybir.dt.uint16
U8 = mybir.dt.uint8
FP8X4 = mybir.dt.float8_e4m3fn_x4
FP4X4 = mybir.dt.float4_e2m1fn_x4
ALU = mybir.AluOpType
ACT = mybir.ActivationFunctionType

P = 128
PACK = 4
BANK = 512
CHUNKS = S // BANK
PER_COL = 16
CHUNK_BYTES = 4 * BANK

BANKS = {"w1": 4, "w2": 2, "w3": 2}
AHEAD = 2
PARTS = [(m0, m0 + P) for m0 in range(0, KEPT, P)]
ON_SCALAR = 2

WORDS_AT = T
STAGE_AT = WORDS_AT + CHUNKS * CHUNK_BYTES
SLICE_BYTES = CHUNKS * CHUNK_BYTES
LARGER_AT = STAGE_AT + PACK * SLICE_BYTES


def load_scale_rows(nc, plane, rows):
    for r in range(4):
        nc.sync.dma_start(out=plane[r:P:32, :].bitcast(I32), in_=rows[r:16:4, :].bitcast(I32))


def entries(lst, first, end):
    return lst[:, first // PER_COL : end // PER_COL]


def chunk(tile, c):
    return tile[:, c * BANK : (c + 1) * BANK]


def tile_list_cartel_bid_screening_kernel(
    tc, tab_words, tab_scales, offs, pos1, pos2, pos3, pos4, w1, w2_words, w2_scales, w3, w4_words, w4_scales, base, out
):
    nc = tc.nc
    with ExitStack() as ctx:
        keep = ctx.enter_context(tc.tile_pool(name="keep", bufs=1))
        ring = ctx.enter_context(tc.tile_pool(name="ring", bufs=2))
        shared = ctx.enter_context(tc.tile_pool(name="shared", bufs=1))
        psum = ctx.enter_context(tc.psum_pool(name="psum", bufs=2))

        idx = keep.tile([P, S // PER_COL], U16, name="idx")
        p1 = keep.tile([P, PAIRS // PER_COL], U16, name="p1")
        p2 = keep.tile([P, PAIRS // PER_COL], U16, name="p2")
        p3 = keep.tile([P, KEPT // PER_COL], U16, name="p3")
        p4 = keep.tile([P, KEPT // PER_COL], U16, name="p4")
        tab_w = keep.tile([P, T], U32, name="tab_w", align_bytes=64)
        tab_s = shared.tile([P, T], U8, name="tab_s", align_bytes=64, offset=0)
        w2_raw = keep.tile([P, 2 * H], U8, name="w2_raw", align_bytes=64)
        w2s_raw = keep.tile([P, H], U8, name="w2s_raw", align_bytes=64)
        w2_w = keep.tile([P, 2 * H], U8, name="w2_w", align_bytes=64)
        w2_s = keep.tile([P, H], U8, name="w2_s", align_bytes=64)
        w4_w = keep.tile([P, N], U32, name="w4_w", align_bytes=64)
        w4_s = keep.tile([P, N], U8, name="w4_s", align_bytes=64)
        bias = keep.tile([P, N // P], F32, name="bias")
        raw = {name: keep.tile([P, PACK, H], F32, name=name + "_raw") for name in ("w1", "w3")}

        nc.vector.memset(tab_s[:].bitcast(I32), 0)
        nc.gpsimd.memset(w2s_raw[:].bitcast(I32), 0)
        nc.gpsimd.memset(w4_s[:].bitcast(I32), 0)

        for lst, src in ((idx, offs), (p2, pos2), (p1, pos1), (p3, pos3), (p4, pos4)):
            nc.sync.dma_start(lst[:], src)
        nc.sync.dma_start(out=raw["w3"][:], in_=w3.rearrange("(p j) r -> p j r", j=PACK))
        load_scale_rows(nc, tab_s, tab_scales[0])
        nc.sync.dma_start(out=raw["w1"][:], in_=w1.rearrange("(p j) r -> p j r", j=PACK))
        nc.sync.dma_start(out=w2_raw[:].bitcast(I32), in_=w2_words[0].bitcast(I32))
        load_scale_rows(nc, w2s_raw, w2_scales[0])
        nc.sync.dma_start(out=tab_w[:].bitcast(I32), in_=tab_words[0].rearrange("p t i -> p (t i)").bitcast(I32))
        nc.sync.dma_start(out=w4_w[:].bitcast(I32), in_=w4_words[0].rearrange("p n i -> p (n i)").bitcast(I32))
        load_scale_rows(nc, w4_s, w4_scales[0])
        with nc.allow_non_contiguous_dma(reason="one value of base for each partition and row tile"):
            nc.sync.dma_start(out=bias[:], in_=base.rearrange("(j p) -> p j", p=P))

        v_s = [keep.tile([P, BANK], U8, name=f"v_s{c}", align_bytes=64) for c in range(CHUNKS)]
        for c in range(CHUNKS):
            nc.vector.tensor_copy(v_s[c][:], tab_s[:].indirect(entries(idx, c * BANK, (c + 1) * BANK)))

        v_w = {}

        def gather_words(c):
            v_w[c] = shared.tile([P, BANK], U32, name=f"v_w{c}", align_bytes=64, offset=WORDS_AT + c * CHUNK_BYTES)
            nc.vector.tensor_copy(v_w[c][:], tab_w[:].indirect(entries(idx, c * BANK, (c + 1) * BANK)))

        for c in range(AHEAD):
            gather_words(c)

        nc.vector.tensor_copy(
            w2_w[:].bitcast(U16).rearrange("p (t q) -> p t q", t=PACK), w2_raw[:].bitcast(U16).rearrange("p (q t) -> p t q", t=PACK)
        )
        nc.vector.tensor_copy(w2_s[:].rearrange("p (t q) -> p t q", t=PACK), w2s_raw[:].rearrange("p (q t) -> p t q", t=PACK))
        stationary = {
            ("w2", t): (w2_w[:, 2 * t * P : 2 * (t + 1) * P].bitcast(FP4X4), w2_s[:, t * P : (t + 1) * P]) for t in range(PACK)
        }

        for half, name in enumerate(("w3", "w1")):
            rounded = keep.tile([P, H * PACK], BF16, name=name + "_rounded", align_bytes=64)
            codes = shared.tile([P, H], U32, name=name + "_codes", align_bytes=64, offset=half * T // 2)
            scales = keep.tile([P, H], U8, name=name + "_scales", align_bytes=64)
            nc.scalar.copy(
                out=rounded[:].rearrange("p (t q j) -> p q t j", t=PACK, j=PACK),
                in_=raw[name][:].rearrange("p j (q t) -> p q t j", t=PACK),
            )
            nc.vector.quantize_mx(out=codes[:].bitcast(FP8X4), scales=scales[:], in_=rounded[:])
            for t in range(PACK):
                stationary[name, t] = (codes[:, t * P : (t + 1) * P].bitcast(FP8X4), scales[:, t * P : (t + 1) * P])

        def product(name, t, c):
            bank = psum.tile([P, BANK], F32, name="bank_" + name, tag=name, bufs=BANKS[name])
            lhs_codes, lhs_scales = stationary[name, t]
            nc.tensor.matmul_mx(
                out=bank[:], lhsT=lhs_codes, lhsT_scale=lhs_scales,
                rhs=v_w[c][:].bitcast(FP8X4), rhs_scale=v_s[c][:], start=True, stop=True,
            )
            return bank

        seconds = {}

        def copy_second(t, c):
            if t == 0 and c + AHEAD < CHUNKS:
                place = WORDS_AT + (c + AHEAD) * CHUNK_BYTES
            else:
                place = STAGE_AT + t * SLICE_BYTES + c * CHUNK_BYTES
            seconds[t, c] = shared.tile([P, BANK], F32, name=f"second{t}_{c}", align_bytes=64, offset=place)
            nc.scalar.copy(out=seconds[t, c][:], in_=product("w2", t, c)[:])

        def maximum(t, c, larger):
            if (t, c) not in seconds:
                copy_second(t, c)
            nc.vector.tensor_tensor(chunk(larger, c), product("w1", t, c)[:], seconds[t, c][:], ALU.max)

        def gated(t, c, larger):
            gate = ring.tile([P, BANK], F32, name="gate", bufs=CHUNKS)
            nc.scalar.activation(out=gate[:], in_=product("w3", t, c)[:], func=ACT.Tanh)
            nc.gpsimd.tensor_tensor(chunk(h[t], c), chunk(larger, c), gate[:], ALU.mult)

        def features(t):
            h[t] = keep.tile([P, S], F32, name=f"h{t}")
            larger = shared.tile([P, S], F32, name=f"larger{t}", align_bytes=64, offset=LARGER_AT + t % 2 * SLICE_BYTES)
            for c in range(CHUNKS):
                if t == 0 and c >= AHEAD:
                    copy_second(1, c - AHEAD)
                maximum(t, c, larger)
                if t == 0:
                    gated(t, c, larger)
                if t == 0 and c + AHEAD < CHUNKS:
                    gather_words(c + AHEAD)
            if t > 0:
                for c in range(CHUNKS):
                    gated(t, c, larger)

        a2 = shared.tile([P, PACK, KEPT], F32, name="a2", align_bytes=64, offset=LARGER_AT + SLICE_BYTES + 4 * PAIRS)
        out_rows = out.rearrange("(j p) m -> p j m", p=P)

        def scores(part):
            m0, m1 = PARTS[part]
            width = m1 - m0
            woven = keep.tile([P, width, PACK], BF16, name=f"woven{part}", align_bytes=64)
            a2_w = keep.tile([P, width], U32, name=f"a2_w{part}", align_bytes=64)
            a2_s = keep.tile([P, width], U8, name=f"a2_s{part}", align_bytes=64)
            by_column = a2[:, :, m0:m1].rearrange("p t m -> p m t")
            if part < len(PARTS) // 2:
                nc.scalar.copy(out=woven[:], in_=by_column)
            else:
                nc.vector.tensor_copy(out=woven[:], in_=by_column)
            nc.vector.quantize_mx(out=a2_w[:].bitcast(FP8X4), scales=a2_s[:], in_=woven[:].rearrange("p m t -> p (m t)"))
            score = keep.tile([P, N // P, width], F32, name=f"score{part}")
            for row_tiles, tag in ((range(ON_SCALAR), "w1"), (range(ON_SCALAR, N // P), ("w2", "w3")[part % 2])):
                bank = psum.tile([P, BANK], F32, name="bank_out", tag=tag, bufs=BANKS[tag])
                for i, j in enumerate(row_tiles):
                    nc.tensor.matmul_mx(
                        out=bank[:, i * width : (i + 1) * width],
                        lhsT=w4_w[:, j * P : (j + 1) * P].bitcast(FP8X4), lhsT_scale=w4_s[:, j * P : (j + 1) * P],
                        rhs=a2_w[:].bitcast(FP8X4), rhs_scale=a2_s[:], start=True, stop=True,
                    )
                for i, j in enumerate(row_tiles):
                    sums = bank[:, i * width : (i + 1) * width]
                    if j < ON_SCALAR:
                        nc.scalar.activation(out=score[:, j, :], in_=sums, func=ACT.Identity, bias=bias[:, j : j + 1])
                    else:
                        nc.vector.tensor_scalar(score[:, j, :], sums, bias[:, j : j + 1], None, ALU.add)
            nc.sync.dma_start(out=out_rows[:, :, m0:m1], in_=score[:])

        def pairs(t):
            last = t == PACK - 1
            a1 = shared.tile([P, PAIRS], F32, name=f"a1_{t}", align_bytes=64, offset=LARGER_AT + min(t + 1, PACK - 1) % 2 * SLICE_BYTES)
            picks = shared.tile([P, S], F32, name=f"picks{t}", align_bytes=64, offset=STAGE_AT + (t + 1) % PACK * SLICE_BYTES)
            for c in range(PAIRS // BANK):
                by_p1 = h[t][:].indirect(entries(p1, c * BANK, (c + 1) * BANK))
                other = chunk(picks, 2 * c)
                nc.vector.tensor_copy(other, h[t][:].indirect(entries(p2, c * BANK, (c + 1) * BANK)))
                if last:
                    nc.vector.tensor_tensor(chunk(a1, c), by_p1, other, ALU.subtract)
                else:
                    first = chunk(picks, 2 * c + 1)
                    nc.vector.tensor_copy(first, by_p1)
                    nc.gpsimd.tensor_tensor(chunk(a1, c), first, other, ALU.subtract)
            kept[t] = keep.tile([P, KEPT], F32, name=f"kept{t}")
            if last:
                size = keep.tile([P, KEPT], F32, name="size_last")
                for part in range(len(PARTS) + 1):
                    if part < len(PARTS):
                        m0, m1 = PARTS[part]
                        nc.vector.tensor_copy(kept[t][:, m0:m1], a1[:].indirect(entries(p3, m0, m1)))
                        nc.scalar.activation(out=size[:, m0:m1], in_=kept[t][:, m0:m1], func=ACT.Abs)
                    if part > 0:
                        m0, m1 = PARTS[part - 1]
                        nc.vector.tensor_tensor(a2[:, t, m0:m1], h[t][:].indirect(entries(p4, m0, m1)), size[:, m0:m1], ALU.add)
                        scores(part - 1)
                return
            if t == 0:
                nc.vector.tensor_copy(incumbent[:], h[t][:].indirect(p4[:]))
            nc.vector.tensor_copy(kept[t][:], a1[:].indirect(p3[:]))
            if t == PACK - 2:
                nc.scalar.activation(out=a2[:, 0, :], in_=kept[0][:], func=ACT.Abs)
                nc.gpsimd.tensor_tensor(a2[:, 0, :], a2[:, 0, :], incumbent[:], ALU.add)
                sizes = shared.tile([P, t, KEPT], F32, name="sizes", align_bytes=64, offset=STAGE_AT + (t + 1) * SLICE_BYTES)
                for earlier in range(1, t + 1):
                    nc.scalar.activation(out=sizes[:, earlier - 1, :], in_=kept[earlier][:], func=ACT.Abs)
                    nc.vector.tensor_tensor(a2[:, earlier, :], h[earlier][:].indirect(p4[:]), sizes[:, earlier - 1, :], ALU.add)

        incumbent = keep.tile([P, KEPT], F32, name="incumbent")
        h, kept = {}, {}
        features(0)
        for t in range(PACK):
            if t + 1 < PACK:
                features(t + 1)
            pairs(t)
